import numpy as np
import ml_dtypes


def mxq(x, axis, fmt="e4m3"):
    dtype, down = {"e4m3": (ml_dtypes.float8_e4m3fn, 7), "e5m2": (ml_dtypes.float8_e5m2, 14)}[fmt]
    v = np.moveaxis(np.asarray(x, np.float32).astype(ml_dtypes.bfloat16).astype(np.float64), axis, -1)
    blocks = v.reshape(v.shape[:-1] + (-1, 32))
    amax = np.abs(blocks).max(-1, keepdims=True)
    byte = np.maximum(np.where(amax > 0, np.frexp(amax)[1] - 1 + 127, 0) - down, 1)
    scale = np.exp2(byte - 127.0)
    codes = (blocks / scale).astype(np.float32).astype(dtype).astype(np.float64)
    return np.moveaxis((codes * scale).reshape(v.shape), -1, axis)


WIDE = False


def mx_kscale(k, group=512):
    if not WIDE:
        return np.ones(k)
    levels = np.array([18, -18])
    if group != 512:
        return np.exp2(np.random.permutation(np.resize(levels, k // group))).repeat(group)
    if k % 512:
        return np.exp2(np.random.permutation(np.resize(levels, k // 32))).repeat(32)
    a = np.empty((k // 512, 16))
    for p in range(k // 512):
        a[p, :8] = np.random.permutation(np.resize(levels, 8))
        for g in range(8):
            far = levels[np.abs(levels - a[p, g]) >= 10]
            a[p, g + 8] = far[np.random.randint(len(far))]
    return np.exp2(a.ravel()).repeat(32)


def f64(x):
    return np.asarray(x).astype(np.float64)


def softplus(v):
    return np.log(1.0 + np.exp(v))


G, D, M, N = 4, 128, 128, 512


def setup_inputs():
    n = np.random.standard_normal
    s_d = mx_kscale(D, 0)
    return {
        "x": (n((G, D, N)) * s_d[:, None]).astype(np.float32),
        "w": (n((D, M)) / np.sqrt(D) / s_d[:, None]).astype(np.float32),
        "b": (0.5 * n((M, 1))).astype(np.float32),
        "tw": (np.random.uniform(0.5, 2.0, (M, 1))).astype(np.float32),
    }


def reference(x, w, b, tw):
    wq = mxq(f64(w), 0, "e4m3")
    xq = mxq(f64(x), 1, "e4m3")
    z = wq.T @ xq
    y = softplus(z + f64(b)) / f64(tw)
    return y

@@ -1,0 +1,107 @@
+import math
+from contextlib import ExitStack
+
+import concourse.mybir as mybir
+
+G, D, M, N = 4, 128, 128, 512
+FLOPS = 2 * G * D * M * N
+
+F32 = mybir.dt.float32
+BF16 = mybir.dt.bfloat16
+U32 = mybir.dt.uint32
+U8 = mybir.dt.uint8
+FP8X4 = mybir.dt.float8_e4m3fn_x4
+ACT = mybir.ActivationFunctionType
+ALU = mybir.AluOpType
+
+P = 128
+PACK = 4
+ROWS = D // PACK
+CW = 128
+CHUNKS = N // CW
+HALF = N // 2
+KNEE = 32.0
+PIECES = [(0, 0, 128), (0, 128, 256), (1, 0, 256), (2, 0, 256), (3, 0, 256), (0, 256, 512), (1, 256, 512), (2, 256, 512), (3, 256, 384), (3, 384, 512)]
+
+
+def tile_rows_mix_pool_kernel(tc, x, w, b, tw, out):
+    nc = tc.nc
+    with ExitStack() as ctx:
+        sb = ctx.enter_context(tc.tile_pool(name="sb", bufs=1))
+        psum = ctx.enter_context(tc.psum_pool(name="psum", bufs=1))
+        ctx.enter_context(tc.manual_schedule())
+
+        w_raw = sb.tile([P, PACK, M], F32)
+        w_rows = w.rearrange("(p j) m -> p j m", j=PACK)
+        b_col = sb.tile([P, 1], F32)
+        tw_col = sb.tile([P, 1], F32)
+        for g, queue in ((0, nc.sync), (2, nc.scalar), (1, nc.sync), (3, nc.scalar)):
+            queue.dma_start(out=w_raw[ROWS * g : ROWS * (g + 1), :, :], in_=w_rows)
+        nc.scalar.dma_start(out=b_col[:], in_=b)
+        x_rows = x.rearrange("g (p j) n -> (g p) j n", j=PACK)
+        x_raw = [sb.tile([P, PACK, CW], F32, name="x_raw%d" % c) for c in range(CHUNKS)]
+        for c in range(CHUNKS):
+            nc.sync.dma_start(out=x_raw[c][:], in_=x_rows[:, :, c * CW : (c + 1) * CW])
+        nc.sync.dma_start(out=tw_col[:], in_=tw)
+
+        zero = sb.tile([P, 1], F32)
+        one = sb.tile([P, 1], F32)
+        warm = sb.tile([P, 1], F32)
+        nc.vector.memset(zero[:], 0.0)
+        nc.vector.memset(one[:], 1.0)
+        nc.scalar.activation(out=warm[:], in_=zero[:], func=ACT.Exp, bias=zero[:], scale=1.0)
+
+        w_bf = sb.tile([P, M, PACK], BF16, align_bytes=64)
+        nc.scalar.activation(out=w_bf[:], in_=w_raw[:].rearrange("p j m -> p m j"), func=ACT.Copy)
+        w_codes = sb.tile([P, M], U32, align_bytes=64)
+        w_scales = sb.tile([P, M], U8, align_bytes=64)
+        nc.vector.quantize_mx(out=w_codes[:].bitcast(FP8X4), scales=w_scales[:], in_=w_bf[:].rearrange("p m j -> p (m j)"))
+
+        z = [[psum.tile([P, N], F32, name="z%d_%d" % (g, h)) for h in range(2)] for g in range(G)]
+        e = sb.tile([P, G, N], F32)
+        t = sb.tile([P, G, N], F32)
+        ec = sb.tile([P, G, N], F32)
+        ln = sb.tile([P, G, N], F32)
+        y = sb.tile([P, G, N], F32)
+        x_bf = [sb.tile([P, CW, PACK], BF16, align_bytes=64, name="x_bf%d" % c) for c in range(CHUNKS)]
+        x_codes = [sb.tile([P, CW], U32, align_bytes=64, name="x_codes%d" % c) for c in range(CHUNKS)]
+        x_scales = [sb.tile([P, CW], U8, align_bytes=64, name="x_scales%d" % c) for c in range(CHUNKS)]
+
+        for c in range(CHUNKS):
+            nc.vector.tensor_copy(out=x_bf[c][:], in_=x_raw[c][:].rearrange("p j n -> p n j"))
+            nc.vector.quantize_mx(out=x_codes[c][:].bitcast(FP8X4), scales=x_scales[c][:], in_=x_bf[c][:].rearrange("p n j -> p (n j)"))
+            place = slice((c % 2) * CW, (c % 2 + 1) * CW)
+            for g in range(G):
+                rows = slice(ROWS * g, ROWS * (g + 1))
+                nc.tensor.matmul_mx(
+                    out=z[g][c // 2][:, place],
+                    lhsT=w_codes[rows, :].bitcast(FP8X4),
+                    lhsT_scale=w_scales[rows, :],
+                    rhs=x_codes[c][rows, :].bitcast(FP8X4),
+                    rhs_scale=x_scales[c][rows, :],
+                    start=True,
+                    stop=True,
+                )
+            for g in range(G):
+                nc.scalar.activation(out=e[:, g, c * CW : (c + 1) * CW], in_=z[g][c // 2][:, place], func=ACT.Exp, bias=b_col[:], scale=1.0)
+
+        warm2 = sb.tile([P, 1], F32)
+        nc.scalar.activation(out=warm2[:], in_=one[:], func=ACT.Ln, bias=zero[:], scale=1.0)
+
+        cap = sb.tile([P, 1], F32)
+        nc.vector.tensor_scalar(out=cap[:], in0=one[:], scalar1=math.exp(KNEE), scalar2=None, op0=ALU.mult)
+        k_col = sb.tile([P, 1], F32)
+        r_col = sb.tile([P, 1], F32)
+        for h in range(2):
+            cols = slice(h * HALF, (h + 1) * HALF)
+            for g in range(G):
+                nc.gpsimd.tensor_scalar(out=ec[:, g, cols], in0=e[:, g, cols], scalar1=cap[:], scalar2=zero[:], op0=ALU.min, op1=ALU.max)
+                nc.vector.tensor_scalar(out=t[:, g, cols], in0=z[g][h][:, 0:HALF], scalar1=b_col[:], scalar2=KNEE, op0=ALU.add, op1=ALU.max)
+            if h == 0:
+                nc.vector.reciprocal(out=r_col[:], in_=tw_col[:])
+        nc.vector.tensor_scalar(out=k_col[:], in0=r_col[:], scalar1=1.0 / KNEE, scalar2=None, op0=ALU.mult)
+
+        for g, lo, hi in PIECES:
+            nc.scalar.activation(out=ln[:, g, lo:hi], in_=ec[:, g, lo:hi], func=ACT.Ln, bias=one[:], scale=1.0)
+            nc.vector.scalar_tensor_tensor(out=y[:, g, lo:hi], in0=ln[:, g, lo:hi], scalar=k_col[:], in1=t[:, g, lo:hi], op0=ALU.mult, op1=ALU.mult)
+            nc.sync.dma_start(out=out[g, :, lo:hi], in_=y[:, g, lo:hi])

@@ -21,6 +21,8 @@ CW = 128
 CHUNKS = N // CW
 HALF = N // 2
 KNEE = 32.0
+ORDER = (0, 2, 1, 3)
+VECTOR_COLS = [80, 128, 64, 128]
 PIECES = [(0, 0, 128), (0, 128, 256), (1, 0, 256), (2, 0, 256), (3, 0, 256), (0, 256, 512), (1, 256, 512), (2, 256, 512), (3, 256, 384), (3, 384, 512)]
 
 
@@ -33,29 +35,30 @@ def tile_rows_mix_pool_kernel(tc, x, w, b, tw, out):
 
         w_raw = sb.tile([P, PACK, M], F32)
         w_rows = w.rearrange("(p j) m -> p j m", j=PACK)
-        b_col = sb.tile([P, 1], F32)
+        rows_in = sb.tile([P, ROWS], F32, align_bytes=64)
+        cols_out = sb.tile([P, ROWS], F32, align_bytes=64)
+        b_col = cols_out[:, 0:1]
         tw_col = sb.tile([P, 1], F32)
+        zero = sb.tile([P, 1], F32)
+        nc.vector.memset(zero[:], 0.0)
+        nc.vector.memset(rows_in[:], 0.0)
         for g, queue in ((0, nc.sync), (2, nc.scalar), (1, nc.sync), (3, nc.scalar)):
             queue.dma_start(out=w_raw[ROWS * g : ROWS * (g + 1), :, :], in_=w_rows)
-        nc.scalar.dma_start(out=b_col[:], in_=b)
         x_rows = x.rearrange("g (p j) n -> (g p) j n", j=PACK)
         x_raw = [sb.tile([P, PACK, CW], F32, name="x_raw%d" % c) for c in range(CHUNKS)]
-        for c in range(CHUNKS):
+        for c in ORDER:
             nc.sync.dma_start(out=x_raw[c][:], in_=x_rows[:, :, c * CW : (c + 1) * CW])
+            if c == ORDER[0]:
+                nc.sync.dma_start(out=rows_in[0:P:ROWS, :], in_=b.rearrange("(q i) o -> q (i o)", i=ROWS))
         nc.sync.dma_start(out=tw_col[:], in_=tw)
 
-        zero = sb.tile([P, 1], F32)
         one = sb.tile([P, 1], F32)
-        warm = sb.tile([P, 1], F32)
-        nc.vector.memset(zero[:], 0.0)
-        nc.vector.memset(one[:], 1.0)
-        nc.scalar.activation(out=warm[:], in_=zero[:], func=ACT.Exp, bias=zero[:], scale=1.0)
+        nc.scalar.activation(out=one[:], in_=zero[:], func=ACT.Exp, bias=zero[:], scale=1.0)
 
         w_bf = sb.tile([P, M, PACK], BF16, align_bytes=64)
-        nc.scalar.activation(out=w_bf[:], in_=w_raw[:].rearrange("p j m -> p m j"), func=ACT.Copy)
+        nc.vector.tensor_copy(out=w_bf[:], in_=w_raw[:].rearrange("p j m -> p m j"))
         w_codes = sb.tile([P, M], U32, align_bytes=64)
         w_scales = sb.tile([P, M], U8, align_bytes=64)
-        nc.vector.quantize_mx(out=w_codes[:].bitcast(FP8X4), scales=w_scales[:], in_=w_bf[:].rearrange("p m j -> p (m j)"))
 
         z = [[psum.tile([P, N], F32, name="z%d_%d" % (g, h)) for h in range(2)] for g in range(G)]
         e = sb.tile([P, G, N], F32)
@@ -67,9 +70,16 @@ def tile_rows_mix_pool_kernel(tc, x, w, b, tw, out):
         x_codes = [sb.tile([P, CW], U32, align_bytes=64, name="x_codes%d" % c) for c in range(CHUNKS)]
         x_scales = [sb.tile([P, CW], U8, align_bytes=64, name="x_scales%d" % c) for c in range(CHUNKS)]
 
-        for c in range(CHUNKS):
-            nc.vector.tensor_copy(out=x_bf[c][:], in_=x_raw[c][:].rearrange("p j n -> p n j"))
+        def interleave(c):
+            split = VECTOR_COLS[c]
+            nc.vector.tensor_copy(out=x_bf[c][:, :split, :], in_=x_raw[c][:, :, :split].rearrange("p j n -> p n j"))
+            if split < CW:
+                nc.scalar.activation(out=x_bf[c][:, split:, :], in_=x_raw[c][:, :, split:].rearrange("p j n -> p n j"), func=ACT.Copy)
+
+        def quantize(c):
             nc.vector.quantize_mx(out=x_codes[c][:].bitcast(FP8X4), scales=x_scales[c][:], in_=x_bf[c][:].rearrange("p n j -> p (n j)"))
+
+        def mix(c):
             place = slice((c % 2) * CW, (c % 2 + 1) * CW)
             for g in range(G):
                 rows = slice(ROWS * g, ROWS * (g + 1))
@@ -83,25 +93,50 @@ def tile_rows_mix_pool_kernel(tc, x, w, b, tw, out):
                     stop=True,
                 )
             for g in range(G):
-                nc.scalar.activation(out=e[:, g, c * CW : (c + 1) * CW], in_=z[g][c // 2][:, place], func=ACT.Exp, bias=b_col[:], scale=1.0)
+                nc.scalar.activation(out=e[:, g, c * CW : (c + 1) * CW], in_=z[g][c // 2][:, place], func=ACT.Exp, bias=b_col, scale=1.0)
 
-        warm2 = sb.tile([P, 1], F32)
-        nc.scalar.activation(out=warm2[:], in_=one[:], func=ACT.Ln, bias=zero[:], scale=1.0)
+        def cap(c):
+            cols = slice(c * CW, (c + 1) * CW)
+            nc.vector.tensor_scalar(out=ec[:, :, cols], in0=e[:, :, cols], scalar1=math.exp(KNEE), scalar2=None, op0=ALU.min)
 
-        cap = sb.tile([P, 1], F32)
-        nc.vector.tensor_scalar(out=cap[:], in0=one[:], scalar1=math.exp(KNEE), scalar2=None, op0=ALU.mult)
+        def slope(g, lo, hi):
+            nc.vector.tensor_scalar(out=t[:, g, lo:hi], in0=z[g][lo // HALF][:, lo % HALF : lo % HALF + hi - lo], scalar1=b_col, scalar2=KNEE, op0=ALU.add, op1=ALU.max)
+
         k_col = sb.tile([P, 1], F32)
         r_col = sb.tile([P, 1], F32)
-        for h in range(2):
-            cols = slice(h * HALF, (h + 1) * HALF)
-            for g in range(G):
-                nc.gpsimd.tensor_scalar(out=ec[:, g, cols], in0=e[:, g, cols], scalar1=cap[:], scalar2=zero[:], op0=ALU.min, op1=ALU.max)
-                nc.vector.tensor_scalar(out=t[:, g, cols], in0=z[g][h][:, 0:HALF], scalar1=b_col[:], scalar2=KNEE, op0=ALU.add, op1=ALU.max)
-            if h == 0:
-                nc.vector.reciprocal(out=r_col[:], in_=tw_col[:])
-        nc.vector.tensor_scalar(out=k_col[:], in0=r_col[:], scalar1=1.0 / KNEE, scalar2=None, op0=ALU.mult)
+
+        c0, c1, c2, c3 = ORDER
+        interleave(c0)
+        nc.vector.transpose(out=cols_out[:], in_=rows_in[:])
+        nc.vector.quantize_mx(out=w_codes[:].bitcast(FP8X4), scales=w_scales[:], in_=w_bf[:].rearrange("p m j -> p (m j)"))
+        quantize(c0)
+        interleave(c1)
+        mix(c0)
+        quantize(c1)
+        mix(c1)
+        interleave(c2)
+        slope(0, 0, CW)
+        slope(1, 0, CW)
+        quantize(c2)
+        mix(c2)
+        interleave(c3)
+        cap(c0)
+        quantize(c3)
+        mix(c3)
+        cap(c1)
+        nc.vector.tensor_scalar(out=r_col[:], in0=tw_col[:], scalar1=KNEE, scalar2=None, op0=ALU.mult)
+        slope(0, CW, HALF)
+        slope(1, CW, HALF)
+        nc.vector.reciprocal(out=k_col[:], in_=r_col[:])
+        cap(c2)
+        slope(2, 0, HALF)
+        slope(3, 0, HALF)
+        cap(c3)
+        for g in range(G):
+            slope(g, HALF, N)
 
         for g, lo, hi in PIECES:
             nc.scalar.activation(out=ln[:, g, lo:hi], in_=ec[:, g, lo:hi], func=ACT.Ln, bias=one[:], scale=1.0)
             nc.vector.scalar_tensor_tensor(out=y[:, g, lo:hi], in0=ln[:, g, lo:hi], scalar=k_col[:], in1=t[:, g, lo:hi], op0=ALU.mult, op1=ALU.mult)
-            nc.sync.dma_start(out=out[g, :, lo:hi], in_=y[:, g, lo:hi])
+            if hi % HALF == 0:
+                nc.sync.dma_start(out=out[g, :, hi - HALF : hi], in_=y[:, g, hi - HALF : hi])

@@ -56,7 +56,7 @@ def tile_rows_mix_pool_kernel(tc, x, w, b, tw, out):
         nc.scalar.activation(out=one[:], in_=zero[:], func=ACT.Exp, bias=zero[:], scale=1.0)
 
         w_bf = sb.tile([P, M, PACK], BF16, align_bytes=64)
-        nc.vector.tensor_copy(out=w_bf[:], in_=w_raw[:].rearrange("p j m -> p m j"))
+        nc.vector.tensor_copy(out=w_bf[:].rearrange("p (m i) j -> p m j i", i=4), in_=w_raw[:].rearrange("p j (m i) -> p m j i", i=4))
         w_codes = sb.tile([P, M], U32, align_bytes=64)
         w_scales = sb.tile([P, M], U8, align_bytes=64)
 
@@ -72,9 +72,9 @@ def tile_rows_mix_pool_kernel(tc, x, w, b, tw, out):
 
         def interleave(c):
             split = VECTOR_COLS[c]
-            nc.vector.tensor_copy(out=x_bf[c][:, :split, :], in_=x_raw[c][:, :, :split].rearrange("p j n -> p n j"))
+            nc.vector.tensor_copy(out=x_bf[c][:, :split, :].rearrange("p (n i) j -> p n j i", i=4), in_=x_raw[c][:, :, :split].rearrange("p j (n i) -> p n j i", i=4))
             if split < CW:
-                nc.scalar.activation(out=x_bf[c][:, split:, :], in_=x_raw[c][:, :, split:].rearrange("p j n -> p n j"), func=ACT.Copy)
+                nc.scalar.activation(out=x_bf[c][:, split:, :].rearrange("p (n i) j -> p n j i", i=4), in_=x_raw[c][:, :, split:].rearrange("p j (n i) -> p n j i", i=4), func=ACT.Copy)
 
         def quantize(c):
             nc.vector.quantize_mx(out=x_codes[c][:].bitcast(FP8X4), scales=x_scales[c][:], in_=x_bf[c][:].rearrange("p n j -> p (n j)"))

@@ -18,12 +18,14 @@ P = 128
 PACK = 4
 ROWS = D // PACK
 CW = 128
-CHUNKS = N // CW
 HALF = N // 2
 KNEE = 32.0
-ORDER = (0, 2, 1, 3)
-VECTOR_COLS = [80, 128, 64, 128]
-PIECES = [(0, 0, 128), (0, 128, 256), (1, 0, 256), (2, 0, 256), (3, 0, 256), (0, 256, 512), (1, 256, 512), (2, 256, 512), (3, 256, 384), (3, 384, 512)]
+CHUNKS = N // CW
+SPLIT = 3 * CW
+W_VECTOR_COLS = 80
+VECTOR_COLS = [64, 128, 128, 64]
+PIECES = [(0, 0, 128), (0, 128, 256), (0, 256, 512), (1, 0, 256), (1, 256, 512), (2, 0, 256), (2, 256, 512), (3, 0, 256), (3, 256, 384), (3, 384, 512)]
+STORES = [(g, lo, lo + HALF) for g in range(G) for lo in (0, HALF)]
 
 
 def tile_rows_mix_pool_kernel(tc, x, w, b, tw, out):
@@ -42,24 +44,32 @@ def tile_rows_mix_pool_kernel(tc, x, w, b, tw, out):
         zero = sb.tile([P, 1], F32)
         nc.vector.memset(zero[:], 0.0)
         nc.vector.memset(rows_in[:], 0.0)
-        for g, queue in ((0, nc.sync), (2, nc.scalar), (1, nc.sync), (3, nc.scalar)):
-            queue.dma_start(out=w_raw[ROWS * g : ROWS * (g + 1), :, :], in_=w_rows)
         x_rows = x.rearrange("g (p j) n -> (g p) j n", j=PACK)
         x_raw = [sb.tile([P, PACK, CW], F32, name="x_raw%d" % c) for c in range(CHUNKS)]
-        for c in ORDER:
-            nc.sync.dma_start(out=x_raw[c][:], in_=x_rows[:, :, c * CW : (c + 1) * CW])
-            if c == ORDER[0]:
-                nc.sync.dma_start(out=rows_in[0:P:ROWS, :], in_=b.rearrange("(q i) o -> q (i o)", i=ROWS))
+
+        def load_w(g, queue):
+            queue.dma_start(out=w_raw[ROWS * g : ROWS * (g + 1), :, :], in_=w_rows)
+
+        def load_x(c, queue):
+            queue.dma_start(out=x_raw[c][:], in_=x_rows[:, :, c * CW : (c + 1) * CW])
+
+        load_w(0, nc.sync)
+        load_w(2, nc.scalar)
+        load_w(1, nc.sync)
+        load_w(3, nc.scalar)
+        load_x(0, nc.sync)
+        nc.sync.dma_start(out=rows_in[0:P:ROWS, :], in_=b.rearrange("(q i) o -> q (i o)", i=ROWS))
+        load_x(3, nc.sync)
+        load_x(1, nc.sync)
+        load_x(2, nc.sync)
         nc.sync.dma_start(out=tw_col[:], in_=tw)
 
         one = sb.tile([P, 1], F32)
         nc.scalar.activation(out=one[:], in_=zero[:], func=ACT.Exp, bias=zero[:], scale=1.0)
 
         w_bf = sb.tile([P, M, PACK], BF16, align_bytes=64)
-        nc.vector.tensor_copy(out=w_bf[:].rearrange("p (m i) j -> p m j i", i=4), in_=w_raw[:].rearrange("p j (m i) -> p m j i", i=4))
         w_codes = sb.tile([P, M], U32, align_bytes=64)
         w_scales = sb.tile([P, M], U8, align_bytes=64)
-
         z = [[psum.tile([P, N], F32, name="z%d_%d" % (g, h)) for h in range(2)] for g in range(G)]
         e = sb.tile([P, G, N], F32)
         t = sb.tile([P, G, N], F32)
@@ -69,74 +79,81 @@ def tile_rows_mix_pool_kernel(tc, x, w, b, tw, out):
         x_bf = [sb.tile([P, CW, PACK], BF16, align_bytes=64, name="x_bf%d" % c) for c in range(CHUNKS)]
         x_codes = [sb.tile([P, CW], U32, align_bytes=64, name="x_codes%d" % c) for c in range(CHUNKS)]
         x_scales = [sb.tile([P, CW], U8, align_bytes=64, name="x_scales%d" % c) for c in range(CHUNKS)]
+        k_col = sb.tile([P, 1], F32)
+        r_col = sb.tile([P, 1], F32)
+
+        def pack(dst, src, split):
+            nc.vector.tensor_copy(out=dst[:, :split, :].rearrange("p (n i) j -> p n j i", i=4), in_=src[:, :, :split].rearrange("p j (n i) -> p n j i", i=4))
+            if split < CW:
+                nc.scalar.activation(out=dst[:, split:, :].rearrange("p (n i) j -> p n j i", i=4), in_=src[:, :, split:].rearrange("p j (n i) -> p n j i", i=4), func=ACT.Copy)
 
         def interleave(c):
-            split = VECTOR_COLS[c]
-            nc.vector.tensor_copy(out=x_bf[c][:, :split, :].rearrange("p (n i) j -> p n j i", i=4), in_=x_raw[c][:, :, :split].rearrange("p j (n i) -> p n j i", i=4))
-            if split < CW:
-                nc.scalar.activation(out=x_bf[c][:, split:, :].rearrange("p (n i) j -> p n j i", i=4), in_=x_raw[c][:, :, split:].rearrange("p j (n i) -> p n j i", i=4), func=ACT.Copy)
+            pack(x_bf[c], x_raw[c], VECTOR_COLS[c])
 
         def quantize(c):
             nc.vector.quantize_mx(out=x_codes[c][:].bitcast(FP8X4), scales=x_scales[c][:], in_=x_bf[c][:].rearrange("p n j -> p (n j)"))
 
-        def mix(c):
-            place = slice((c % 2) * CW, (c % 2 + 1) * CW)
+        def quantize_w():
+            nc.vector.quantize_mx(out=w_codes[:].bitcast(FP8X4), scales=w_scales[:], in_=w_bf[:].rearrange("p m j -> p (m j)"))
+
+        def sums(g, lo, hi):
+            return z[g][lo // SPLIT][:, lo % SPLIT : lo % SPLIT + hi - lo]
+
+        def mix(*chunks):
             for g in range(G):
                 rows = slice(ROWS * g, ROWS * (g + 1))
-                nc.tensor.matmul_mx(
-                    out=z[g][c // 2][:, place],
-                    lhsT=w_codes[rows, :].bitcast(FP8X4),
-                    lhsT_scale=w_scales[rows, :],
-                    rhs=x_codes[c][rows, :].bitcast(FP8X4),
-                    rhs_scale=x_scales[c][rows, :],
-                    start=True,
-                    stop=True,
-                )
-            for g in range(G):
-                nc.scalar.activation(out=e[:, g, c * CW : (c + 1) * CW], in_=z[g][c // 2][:, place], func=ACT.Exp, bias=b_col, scale=1.0)
+                for c in chunks:
+                    nc.tensor.matmul_mx(
+                        out=sums(g, c * CW, (c + 1) * CW),
+                        lhsT=w_codes[rows, :].bitcast(FP8X4),
+                        lhsT_scale=w_scales[rows, :],
+                        rhs=x_codes[c][rows, :].bitcast(FP8X4),
+                        rhs_scale=x_scales[c][rows, :],
+                        start=True,
+                        stop=True,
+                    )
 
-        def cap(c):
-            cols = slice(c * CW, (c + 1) * CW)
-            nc.vector.tensor_scalar(out=ec[:, :, cols], in0=e[:, :, cols], scalar1=math.exp(KNEE), scalar2=None, op0=ALU.min)
+        def exps(lo, hi):
+            for g in range(G):
+                nc.scalar.activation(out=e[:, g, lo:hi], in_=sums(g, lo, hi), func=ACT.Exp, bias=b_col, scale=1.0)
+
+        def cap(lo, hi):
+            nc.vector.tensor_scalar(out=ec[:, :, lo:hi], in0=e[:, :, lo:hi], scalar1=math.exp(KNEE), scalar2=None, op0=ALU.min)
 
         def slope(g, lo, hi):
-            nc.vector.tensor_scalar(out=t[:, g, lo:hi], in0=z[g][lo // HALF][:, lo % HALF : lo % HALF + hi - lo], scalar1=b_col, scalar2=KNEE, op0=ALU.add, op1=ALU.max)
+            nc.vector.tensor_scalar(out=t[:, g, lo:hi], in0=sums(g, lo, hi), scalar1=b_col, scalar2=KNEE, op0=ALU.add, op1=ALU.max)
 
-        k_col = sb.tile([P, 1], F32)
-        r_col = sb.tile([P, 1], F32)
-
-        c0, c1, c2, c3 = ORDER
-        interleave(c0)
+        pack(w_bf, w_raw, W_VECTOR_COLS)
+        interleave(0)
+        quantize_w()
+        quantize(0)
         nc.vector.transpose(out=cols_out[:], in_=rows_in[:])
-        nc.vector.quantize_mx(out=w_codes[:].bitcast(FP8X4), scales=w_scales[:], in_=w_bf[:].rearrange("p m j -> p (m j)"))
-        quantize(c0)
-        interleave(c1)
-        mix(c0)
-        quantize(c1)
-        mix(c1)
-        interleave(c2)
-        slope(0, 0, CW)
-        slope(1, 0, CW)
-        quantize(c2)
-        mix(c2)
-        interleave(c3)
-        cap(c0)
-        quantize(c3)
-        mix(c3)
-        cap(c1)
+        interleave(3)
+        mix(0)
+        exps(0, CW)
+        quantize(3)
+        mix(3)
+        exps(SPLIT, N)
+        interleave(1)
+        interleave(2)
+        quantize(1)
+        quantize(2)
+        mix(1, 2)
+        exps(CW, SPLIT)
         nc.vector.tensor_scalar(out=r_col[:], in0=tw_col[:], scalar1=KNEE, scalar2=None, op0=ALU.mult)
-        slope(0, CW, HALF)
-        slope(1, CW, HALF)
+        cap(0, CW)
         nc.vector.reciprocal(out=k_col[:], in_=r_col[:])
-        cap(c2)
-        slope(2, 0, HALF)
-        slope(3, 0, HALF)
-        cap(c3)
         for g in range(G):
-            slope(g, HALF, N)
+            slope(g, SPLIT, N)
+        cap(SPLIT, N)
+        for g in range(G - 1):
+            slope(g, 0, SPLIT)
+        cap(CW, SPLIT)
+        slope(G - 1, 0, SPLIT)
 
         for g, lo, hi in PIECES:
             nc.scalar.activation(out=ln[:, g, lo:hi], in_=ec[:, g, lo:hi], func=ACT.Ln, bias=one[:], scale=1.0)
             nc.vector.scalar_tensor_tensor(out=y[:, g, lo:hi], in0=ln[:, g, lo:hi], scalar=k_col[:], in1=t[:, g, lo:hi], op0=ALU.mult, op1=ALU.mult)
-            if hi % HALF == 0:
-                nc.sync.dma_start(out=out[g, :, hi - HALF : hi], in_=y[:, g, hi - HALF : hi])
+            for sg, slo, shi in STORES:
+                if sg == g and shi == hi:
+                    nc.sync.dma_start(out=out[g, :, slo:shi], in_=y[:, g, slo:shi])

@@ -25,7 +25,7 @@ SPLIT = 3 * CW
 W_VECTOR_COLS = 80
 VECTOR_COLS = [64, 128, 128, 64]
 PIECES = [(0, 0, 128), (0, 128, 256), (0, 256, 512), (1, 0, 256), (1, 256, 512), (2, 0, 256), (2, 256, 512), (3, 0, 256), (3, 256, 384), (3, 384, 512)]
-STORES = [(g, lo, lo + HALF) for g in range(G) for lo in (0, HALF)]
+STORES = PIECES
 
 
 def tile_rows_mix_pool_kernel(tc, x, w, b, tw, out):

@@ -18,14 +18,19 @@ P = 128
 PACK = 4
 ROWS = D // PACK
 CW = 128
-HALF = N // 2
-KNEE = 32.0
 CHUNKS = N // CW
-SPLIT = 3 * CW
+HALF = N // 2
+LINE = 4
+KNEE = 32.0
+
+SPLIT = (CHUNKS - 1) * CW
+FIRST, MIDDLE_A, MIDDLE_B, LAST = range(CHUNKS)
+
 W_VECTOR_COLS = 80
-VECTOR_COLS = [64, 128, 128, 64]
-PIECES = [(0, 0, 128), (0, 128, 256), (0, 256, 512), (1, 0, 256), (1, 256, 512), (2, 0, 256), (2, 256, 512), (3, 0, 256), (3, 256, 384), (3, 384, 512)]
-STORES = PIECES
+VECTOR_COLS = {FIRST: 64, LAST: 32, MIDDLE_A: CW, MIDDLE_B: CW}
+
+HALVES = [(g, lo, lo + HALF) for g in range(G) for lo in (0, HALF)]
+PIECES = [(0, 0, CW), (0, CW, HALF)] + HALVES[1:-1] + [(G - 1, HALF, N - CW), (G - 1, N - CW, N)]
 
 
 def tile_rows_mix_pool_kernel(tc, x, w, b, tw, out):
@@ -37,31 +42,25 @@ def tile_rows_mix_pool_kernel(tc, x, w, b, tw, out):
 
         w_raw = sb.tile([P, PACK, M], F32)
         w_rows = w.rearrange("(p j) m -> p j m", j=PACK)
-        rows_in = sb.tile([P, ROWS], F32, align_bytes=64)
-        cols_out = sb.tile([P, ROWS], F32, align_bytes=64)
-        b_col = cols_out[:, 0:1]
+        b_rows = sb.tile([P, ROWS], F32, align_bytes=64)
+        b_turned = sb.tile([P, ROWS], F32, align_bytes=64)
+        b_col = b_turned[:, 0:1]
         tw_col = sb.tile([P, 1], F32)
         zero = sb.tile([P, 1], F32)
         nc.vector.memset(zero[:], 0.0)
-        nc.vector.memset(rows_in[:], 0.0)
+        nc.vector.memset(b_rows[:], 0.0)
         x_rows = x.rearrange("g (p j) n -> (g p) j n", j=PACK)
         x_raw = [sb.tile([P, PACK, CW], F32, name="x_raw%d" % c) for c in range(CHUNKS)]
 
-        def load_w(g, queue):
+        def load_x(c):
+            nc.sync.dma_start(out=x_raw[c][:], in_=x_rows[:, :, c * CW : (c + 1) * CW])
+
+        for g, queue in ((0, nc.sync), (2, nc.scalar), (1, nc.sync), (3, nc.scalar)):
             queue.dma_start(out=w_raw[ROWS * g : ROWS * (g + 1), :, :], in_=w_rows)
-
-        def load_x(c, queue):
-            queue.dma_start(out=x_raw[c][:], in_=x_rows[:, :, c * CW : (c + 1) * CW])
-
-        load_w(0, nc.sync)
-        load_w(2, nc.scalar)
-        load_w(1, nc.sync)
-        load_w(3, nc.scalar)
-        load_x(0, nc.sync)
-        nc.sync.dma_start(out=rows_in[0:P:ROWS, :], in_=b.rearrange("(q i) o -> q (i o)", i=ROWS))
-        load_x(3, nc.sync)
-        load_x(1, nc.sync)
-        load_x(2, nc.sync)
+        load_x(FIRST)
+        nc.sync.dma_start(out=b_rows[0:P:ROWS, :], in_=b.rearrange("(q i) o -> q (i o)", i=ROWS))
+        for c in (LAST, MIDDLE_A, MIDDLE_B):
+            load_x(c)
         nc.sync.dma_start(out=tw_col[:], in_=tw)
 
         one = sb.tile([P, 1], F32)
@@ -72,34 +71,41 @@ def tile_rows_mix_pool_kernel(tc, x, w, b, tw, out):
         w_scales = sb.tile([P, M], U8, align_bytes=64)
         z = [[psum.tile([P, N], F32, name="z%d_%d" % (g, h)) for h in range(2)] for g in range(G)]
         e = sb.tile([P, G, N], F32)
-        t = sb.tile([P, G, N], F32)
-        ec = sb.tile([P, G, N], F32)
+        v_high = sb.tile([P, G, N], F32)
+        e_capped = sb.tile([P, G, N], F32)
         ln = sb.tile([P, G, N], F32)
         y = sb.tile([P, G, N], F32)
         x_bf = [sb.tile([P, CW, PACK], BF16, align_bytes=64, name="x_bf%d" % c) for c in range(CHUNKS)]
         x_codes = [sb.tile([P, CW], U32, align_bytes=64, name="x_codes%d" % c) for c in range(CHUNKS)]
         x_scales = [sb.tile([P, CW], U8, align_bytes=64, name="x_scales%d" % c) for c in range(CHUNKS)]
-        k_col = sb.tile([P, 1], F32)
-        r_col = sb.tile([P, 1], F32)
+        inv_col = sb.tile([P, 1], F32)
+        knee_tw_col = sb.tile([P, 1], F32)
 
         def pack(dst, src, split):
-            nc.vector.tensor_copy(out=dst[:, :split, :].rearrange("p (n i) j -> p n j i", i=4), in_=src[:, :, :split].rearrange("p j (n i) -> p n j i", i=4))
+            nc.vector.tensor_copy(
+                out=dst[:, :split, :].rearrange("p (n i) j -> p n j i", i=LINE),
+                in_=src[:, :, :split].rearrange("p j (n i) -> p n j i", i=LINE),
+            )
             if split < CW:
-                nc.scalar.activation(out=dst[:, split:, :].rearrange("p (n i) j -> p n j i", i=4), in_=src[:, :, split:].rearrange("p j (n i) -> p n j i", i=4), func=ACT.Copy)
+                nc.scalar.activation(
+                    out=dst[:, split:, :].rearrange("p (n i) j -> p n j i", i=LINE),
+                    in_=src[:, :, split:].rearrange("p j (n i) -> p n j i", i=LINE),
+                    func=ACT.Copy,
+                )
 
         def interleave(c):
             pack(x_bf[c], x_raw[c], VECTOR_COLS[c])
 
-        def quantize(c):
-            nc.vector.quantize_mx(out=x_codes[c][:].bitcast(FP8X4), scales=x_scales[c][:], in_=x_bf[c][:].rearrange("p n j -> p (n j)"))
+        def quantize(codes, scales, packed):
+            nc.vector.quantize_mx(out=codes[:].bitcast(FP8X4), scales=scales[:], in_=packed[:].rearrange("p n j -> p (n j)"))
 
-        def quantize_w():
-            nc.vector.quantize_mx(out=w_codes[:].bitcast(FP8X4), scales=w_scales[:], in_=w_bf[:].rearrange("p m j -> p (m j)"))
+        def quantize_x(c):
+            quantize(x_codes[c], x_scales[c], x_bf[c])
 
         def sums(g, lo, hi):
             return z[g][lo // SPLIT][:, lo % SPLIT : lo % SPLIT + hi - lo]
 
-        def mix(*chunks):
+        def mix_and_exp(*chunks):
             for g in range(G):
                 rows = slice(ROWS * g, ROWS * (g + 1))
                 for c in chunks:
@@ -112,48 +118,45 @@ def tile_rows_mix_pool_kernel(tc, x, w, b, tw, out):
                         start=True,
                         stop=True,
                     )
-
-        def exps(lo, hi):
+            lo, hi = chunks[0] * CW, (chunks[-1] + 1) * CW
             for g in range(G):
                 nc.scalar.activation(out=e[:, g, lo:hi], in_=sums(g, lo, hi), func=ACT.Exp, bias=b_col, scale=1.0)
 
         def cap(lo, hi):
-            nc.vector.tensor_scalar(out=ec[:, :, lo:hi], in0=e[:, :, lo:hi], scalar1=math.exp(KNEE), scalar2=None, op0=ALU.min)
+            nc.vector.tensor_scalar(out=e_capped[:, :, lo:hi], in0=e[:, :, lo:hi], scalar1=math.exp(KNEE), scalar2=None, op0=ALU.min)
 
-        def slope(g, lo, hi):
-            nc.vector.tensor_scalar(out=t[:, g, lo:hi], in0=sums(g, lo, hi), scalar1=b_col, scalar2=KNEE, op0=ALU.add, op1=ALU.max)
+        def high(g, lo, hi):
+            nc.vector.tensor_scalar(out=v_high[:, g, lo:hi], in0=sums(g, lo, hi), scalar1=b_col, scalar2=KNEE, op0=ALU.add, op1=ALU.max)
 
         pack(w_bf, w_raw, W_VECTOR_COLS)
-        interleave(0)
-        quantize_w()
-        quantize(0)
-        nc.vector.transpose(out=cols_out[:], in_=rows_in[:])
-        interleave(3)
-        mix(0)
-        exps(0, CW)
-        quantize(3)
-        mix(3)
-        exps(SPLIT, N)
-        interleave(1)
-        interleave(2)
-        quantize(1)
-        quantize(2)
-        mix(1, 2)
-        exps(CW, SPLIT)
-        nc.vector.tensor_scalar(out=r_col[:], in0=tw_col[:], scalar1=KNEE, scalar2=None, op0=ALU.mult)
+        interleave(FIRST)
+        quantize(w_codes, w_scales, w_bf)
+        quantize_x(FIRST)
+        nc.vector.transpose(out=b_turned[:], in_=b_rows[:])
+        interleave(LAST)
+        mix_and_exp(FIRST)
+        interleave(MIDDLE_A)
+        quantize_x(LAST)
+        mix_and_exp(LAST)
+        interleave(MIDDLE_B)
+        quantize_x(MIDDLE_A)
+        quantize_x(MIDDLE_B)
+        mix_and_exp(MIDDLE_A, MIDDLE_B)
+
+        nc.vector.tensor_scalar(out=knee_tw_col[:], in0=tw_col[:], scalar1=KNEE, scalar2=None, op0=ALU.mult)
         cap(0, CW)
-        nc.vector.reciprocal(out=k_col[:], in_=r_col[:])
+        nc.vector.reciprocal(out=inv_col[:], in_=knee_tw_col[:])
         for g in range(G):
-            slope(g, SPLIT, N)
+            high(g, SPLIT, N)
         cap(SPLIT, N)
         for g in range(G - 1):
-            slope(g, 0, SPLIT)
+            high(g, 0, SPLIT)
         cap(CW, SPLIT)
-        slope(G - 1, 0, SPLIT)
+        high(G - 1, 0, SPLIT)
 
         for g, lo, hi in PIECES:
-            nc.scalar.activation(out=ln[:, g, lo:hi], in_=ec[:, g, lo:hi], func=ACT.Ln, bias=one[:], scale=1.0)
-            nc.vector.scalar_tensor_tensor(out=y[:, g, lo:hi], in0=ln[:, g, lo:hi], scalar=k_col[:], in1=t[:, g, lo:hi], op0=ALU.mult, op1=ALU.mult)
-            for sg, slo, shi in STORES:
-                if sg == g and shi == hi:
-                    nc.sync.dma_start(out=out[g, :, slo:shi], in_=y[:, g, slo:shi])
+            nc.scalar.activation(out=ln[:, g, lo:hi], in_=e_capped[:, g, lo:hi], func=ACT.Ln, bias=one[:], scale=1.0)
+            nc.vector.scalar_tensor_tensor(
+                out=y[:, g, lo:hi], in0=ln[:, g, lo:hi], scalar=inv_col[:], in1=v_high[:, g, lo:hi], op0=ALU.mult, op1=ALU.mult
+            )
+            nc.sync.dma_start(out=out[g, :, lo:hi], in_=y[:, g, lo:hi])

@@ -29,8 +29,7 @@ FIRST, MIDDLE_A, MIDDLE_B, LAST = range(CHUNKS)
 W_VECTOR_COLS = 80
 VECTOR_COLS = {FIRST: 64, LAST: 32, MIDDLE_A: CW, MIDDLE_B: CW}
 
-HALVES = [(g, lo, lo + HALF) for g in range(G) for lo in (0, HALF)]
-PIECES = [(0, 0, CW), (0, CW, HALF)] + HALVES[1:-1] + [(G - 1, HALF, N - CW), (G - 1, N - CW, N)]
+STORE_COLS = [HALF] + [N] * (G - 1)
 
 
 def tile_rows_mix_pool_kernel(tc, x, w, b, tw, out):
@@ -154,9 +153,12 @@ def tile_rows_mix_pool_kernel(tc, x, w, b, tw, out):
         cap(CW, SPLIT)
         high(G - 1, 0, SPLIT)
 
-        for g, lo, hi in PIECES:
-            nc.scalar.activation(out=ln[:, g, lo:hi], in_=e_capped[:, g, lo:hi], func=ACT.Ln, bias=one[:], scale=1.0)
-            nc.vector.scalar_tensor_tensor(
-                out=y[:, g, lo:hi], in0=ln[:, g, lo:hi], scalar=inv_col[:], in1=v_high[:, g, lo:hi], op0=ALU.mult, op1=ALU.mult
-            )
-            nc.sync.dma_start(out=out[g, :, lo:hi], in_=y[:, g, lo:hi])
+        for g in range(G):
+            for lo in (0, HALF):
+                hi = lo + HALF
+                nc.scalar.activation(out=ln[:, g, lo:hi], in_=e_capped[:, g, lo:hi], func=ACT.Ln, bias=one[:], scale=1.0)
+                nc.vector.scalar_tensor_tensor(
+                    out=y[:, g, lo:hi], in0=ln[:, g, lo:hi], scalar=inv_col[:], in1=v_high[:, g, lo:hi], op0=ALU.mult, op1=ALU.mult
+                )
+                if hi % STORE_COLS[g] == 0:
+                    nc.sync.dma_start(out=out[g, :, hi - STORE_COLS[g] : hi], in_=y[:, g, hi - STORE_COLS[g] : hi])

@@ -26,7 +26,6 @@ KNEE = 32.0
 SPLIT = (CHUNKS - 1) * CW
 FIRST, MIDDLE_A, MIDDLE_B, LAST = range(CHUNKS)
 
-W_VECTOR_COLS = 80
 VECTOR_COLS = {FIRST: 64, LAST: 32, MIDDLE_A: CW, MIDDLE_B: CW}
 
 STORE_COLS = [HALF] + [N] * (G - 1)
@@ -127,7 +126,7 @@ def tile_rows_mix_pool_kernel(tc, x, w, b, tw, out):
         def high(g, lo, hi):
             nc.vector.tensor_scalar(out=v_high[:, g, lo:hi], in0=sums(g, lo, hi), scalar1=b_col, scalar2=KNEE, op0=ALU.add, op1=ALU.max)
 
-        pack(w_bf, w_raw, W_VECTOR_COLS)
+        pack(w_bf, w_raw, M)
         interleave(FIRST)
         quantize(w_codes, w_scales, w_bf)
         quantize_x(FIRST)

@@ -103,21 +103,22 @@ def tile_rows_mix_pool_kernel(tc, x, w, b, tw, out):
         def sums(g, lo, hi):
             return z[g][lo // SPLIT][:, lo % SPLIT : lo % SPLIT + hi - lo]
 
-        def mix_and_exp(*chunks):
-            for g in range(G):
+        def mix(c, samples):
+            for g in samples:
                 rows = slice(ROWS * g, ROWS * (g + 1))
-                for c in chunks:
-                    nc.tensor.matmul_mx(
-                        out=sums(g, c * CW, (c + 1) * CW),
-                        lhsT=w_codes[rows, :].bitcast(FP8X4),
-                        lhsT_scale=w_scales[rows, :],
-                        rhs=x_codes[c][rows, :].bitcast(FP8X4),
-                        rhs_scale=x_scales[c][rows, :],
-                        start=True,
-                        stop=True,
-                    )
-            lo, hi = chunks[0] * CW, (chunks[-1] + 1) * CW
-            for g in range(G):
+                nc.tensor.matmul_mx(
+                    out=sums(g, c * CW, (c + 1) * CW),
+                    lhsT=w_codes[rows, :].bitcast(FP8X4),
+                    lhsT_scale=w_scales[rows, :],
+                    rhs=x_codes[c][rows, :].bitcast(FP8X4),
+                    rhs_scale=x_scales[c][rows, :],
+                    start=True,
+                    stop=True,
+                )
+
+        def exp(first, last, samples):
+            lo, hi = first * CW, (last + 1) * CW
+            for g in samples:
                 nc.scalar.activation(out=e[:, g, lo:hi], in_=sums(g, lo, hi), func=ACT.Exp, bias=b_col, scale=1.0)
 
         def cap(lo, hi):
@@ -132,14 +133,21 @@ def tile_rows_mix_pool_kernel(tc, x, w, b, tw, out):
         quantize_x(FIRST)
         nc.vector.transpose(out=b_turned[:], in_=b_rows[:])
         interleave(LAST)
-        mix_and_exp(FIRST)
+        mix(FIRST, range(G))
+        exp(FIRST, FIRST, range(G))
         interleave(MIDDLE_A)
         quantize_x(LAST)
-        mix_and_exp(LAST)
+        mix(LAST, range(G))
+        exp(LAST, LAST, range(G))
         interleave(MIDDLE_B)
+        others, final = range(G - 1), [G - 1]
         quantize_x(MIDDLE_A)
+        mix(MIDDLE_A, reversed(range(G)))
+        exp(MIDDLE_A, MIDDLE_A, final)
         quantize_x(MIDDLE_B)
-        mix_and_exp(MIDDLE_A, MIDDLE_B)
+        mix(MIDDLE_B, range(G))
+        exp(MIDDLE_A, MIDDLE_B, others)
+        exp(MIDDLE_B, MIDDLE_B, final)
 
         nc.vector.tensor_scalar(out=knee_tw_col[:], in0=tw_col[:], scalar1=KNEE, scalar2=None, op0=ALU.mult)
         cap(0, CW)

@@ -21,6 +21,7 @@ CW = 128
 CHUNKS = N // CW
 HALF = N // 2
 LINE = 4
+DMA_ALIGN = 256
 KNEE = 32.0
 
 SPLIT = (CHUNKS - 1) * CW
@@ -38,7 +39,7 @@ def tile_rows_mix_pool_kernel(tc, x, w, b, tw, out):
         psum = ctx.enter_context(tc.psum_pool(name="psum", bufs=1))
         ctx.enter_context(tc.manual_schedule())
 
-        w_raw = sb.tile([P, PACK, M], F32)
+        w_raw = sb.tile([P, PACK, M], F32, align_bytes=DMA_ALIGN)
         w_rows = w.rearrange("(p j) m -> p j m", j=PACK)
         b_rows = sb.tile([P, ROWS], F32, align_bytes=64)
         b_turned = sb.tile([P, ROWS], F32, align_bytes=64)
@@ -48,7 +49,7 @@ def tile_rows_mix_pool_kernel(tc, x, w, b, tw, out):
         nc.vector.memset(zero[:], 0.0)
         nc.vector.memset(b_rows[:], 0.0)
         x_rows = x.rearrange("g (p j) n -> (g p) j n", j=PACK)
-        x_raw = [sb.tile([P, PACK, CW], F32, name="x_raw%d" % c) for c in range(CHUNKS)]
+        x_raw = [sb.tile([P, PACK, CW], F32, align_bytes=DMA_ALIGN, name="x_raw%d" % c) for c in range(CHUNKS)]
 
         def load_x(c):
             nc.sync.dma_start(out=x_raw[c][:], in_=x_rows[:, :, c * CW : (c + 1) * CW])
@@ -72,7 +73,7 @@ def tile_rows_mix_pool_kernel(tc, x, w, b, tw, out):
         v_high = sb.tile([P, G, N], F32)
         e_capped = sb.tile([P, G, N], F32)
         ln = sb.tile([P, G, N], F32)
-        y = sb.tile([P, G, N], F32)
+        y = sb.tile([P, G, N], F32, align_bytes=DMA_ALIGN)
         x_bf = [sb.tile([P, CW, PACK], BF16, align_bytes=64, name="x_bf%d" % c) for c in range(CHUNKS)]
         x_codes = [sb.tile([P, CW], U32, align_bytes=64, name="x_codes%d" % c) for c in range(CHUNKS)]
         x_scales = [sb.tile([P, CW], U8, align_bytes=64, name="x_scales%d" % c) for c in range(CHUNKS)]

import math
from contextlib import ExitStack

import concourse.mybir as mybir

G, D, M, N = 4, 128, 128, 512
FLOPS = 2 * G * D * M * N

F32 = mybir.dt.float32
BF16 = mybir.dt.bfloat16
U32 = mybir.dt.uint32
U8 = mybir.dt.uint8
FP8X4 = mybir.dt.float8_e4m3fn_x4
ACT = mybir.ActivationFunctionType
ALU = mybir.AluOpType

P = 128
PACK = 4
ROWS = D // PACK
CW = 128
CHUNKS = N // CW
HALF = N // 2
LINE = 4
DMA_ALIGN = 256
KNEE = 32.0

SPLIT = (CHUNKS - 1) * CW
FIRST, MIDDLE_A, MIDDLE_B, LAST = range(CHUNKS)

VECTOR_COLS = {FIRST: 64, LAST: 32, MIDDLE_A: CW, MIDDLE_B: CW}

STORE_COLS = [HALF] + [N] * (G - 1)


def tile_rows_mix_pool_kernel(tc, x, w, b, tw, out):
    nc = tc.nc
    with ExitStack() as ctx:
        sb = ctx.enter_context(tc.tile_pool(name="sb", bufs=1))
        psum = ctx.enter_context(tc.psum_pool(name="psum", bufs=1))
        ctx.enter_context(tc.manual_schedule())

        w_raw = sb.tile([P, PACK, M], F32, align_bytes=DMA_ALIGN)
        w_rows = w.rearrange("(p j) m -> p j m", j=PACK)
        b_rows = sb.tile([P, ROWS], F32, align_bytes=64)
        b_turned = sb.tile([P, ROWS], F32, align_bytes=64)
        b_col = b_turned[:, 0:1]
        tw_col = sb.tile([P, 1], F32)
        zero = sb.tile([P, 1], F32)
        nc.vector.memset(zero[:], 0.0)
        nc.vector.memset(b_rows[:], 0.0)
        x_rows = x.rearrange("g (p j) n -> (g p) j n", j=PACK)
        x_raw = [sb.tile([P, PACK, CW], F32, align_bytes=DMA_ALIGN, name="x_raw%d" % c) for c in range(CHUNKS)]

        def load_x(c):
            nc.sync.dma_start(out=x_raw[c][:], in_=x_rows[:, :, c * CW : (c + 1) * CW])

        for g, queue in ((0, nc.sync), (2, nc.scalar), (1, nc.sync), (3, nc.scalar)):
            queue.dma_start(out=w_raw[ROWS * g : ROWS * (g + 1), :, :], in_=w_rows)
        load_x(FIRST)
        nc.sync.dma_start(out=b_rows[0:P:ROWS, :], in_=b.rearrange("(q i) o -> q (i o)", i=ROWS))
        for c in (LAST, MIDDLE_A, MIDDLE_B):
            load_x(c)
        nc.sync.dma_start(out=tw_col[:], in_=tw)

        one = sb.tile([P, 1], F32)
        nc.scalar.activation(out=one[:], in_=zero[:], func=ACT.Exp, bias=zero[:], scale=1.0)

        w_bf = sb.tile([P, M, PACK], BF16, align_bytes=64)
        w_codes = sb.tile([P, M], U32, align_bytes=64)
        w_scales = sb.tile([P, M], U8, align_bytes=64)
        z = [[psum.tile([P, N], F32, name="z%d_%d" % (g, h)) for h in range(2)] for g in range(G)]
        e = sb.tile([P, G, N], F32)
        v_high = sb.tile([P, G, N], F32)
        e_capped = sb.tile([P, G, N], F32)
        ln = sb.tile([P, G, N], F32)
        y = sb.tile([P, G, N], F32, align_bytes=DMA_ALIGN)
        x_bf = [sb.tile([P, CW, PACK], BF16, align_bytes=64, name="x_bf%d" % c) for c in range(CHUNKS)]
        x_codes = [sb.tile([P, CW], U32, align_bytes=64, name="x_codes%d" % c) for c in range(CHUNKS)]
        x_scales = [sb.tile([P, CW], U8, align_bytes=64, name="x_scales%d" % c) for c in range(CHUNKS)]
        inv_col = sb.tile([P, 1], F32)
        knee_tw_col = sb.tile([P, 1], F32)

        def pack(dst, src, split):
            nc.vector.tensor_copy(
                out=dst[:, :split, :].rearrange("p (n i) j -> p n j i", i=LINE),
                in_=src[:, :, :split].rearrange("p j (n i) -> p n j i", i=LINE),
            )
            if split < CW:
                nc.scalar.activation(
                    out=dst[:, split:, :].rearrange("p (n i) j -> p n j i", i=LINE),
                    in_=src[:, :, split:].rearrange("p j (n i) -> p n j i", i=LINE),
                    func=ACT.Copy,
                )

        def interleave(c):
            pack(x_bf[c], x_raw[c], VECTOR_COLS[c])

        def quantize(codes, scales, packed):
            nc.vector.quantize_mx(out=codes[:].bitcast(FP8X4), scales=scales[:], in_=packed[:].rearrange("p n j -> p (n j)"))

        def quantize_x(c):
            quantize(x_codes[c], x_scales[c], x_bf[c])

        def sums(g, lo, hi):
            return z[g][lo // SPLIT][:, lo % SPLIT : lo % SPLIT + hi - lo]

        def mix(c, samples):
            for g in samples:
                rows = slice(ROWS * g, ROWS * (g + 1))
                nc.tensor.matmul_mx(
                    out=sums(g, c * CW, (c + 1) * CW),
                    lhsT=w_codes[rows, :].bitcast(FP8X4),
                    lhsT_scale=w_scales[rows, :],
                    rhs=x_codes[c][rows, :].bitcast(FP8X4),
                    rhs_scale=x_scales[c][rows, :],
                    start=True,
                    stop=True,
                )

        def exp(first, last, samples):
            lo, hi = first * CW, (last + 1) * CW
            for g in samples:
                nc.scalar.activation(out=e[:, g, lo:hi], in_=sums(g, lo, hi), func=ACT.Exp, bias=b_col, scale=1.0)

        def cap(lo, hi):
            nc.vector.tensor_scalar(out=e_capped[:, :, lo:hi], in0=e[:, :, lo:hi], scalar1=math.exp(KNEE), scalar2=None, op0=ALU.min)

        def high(g, lo, hi):
            nc.vector.tensor_scalar(out=v_high[:, g, lo:hi], in0=sums(g, lo, hi), scalar1=b_col, scalar2=KNEE, op0=ALU.add, op1=ALU.max)

        pack(w_bf, w_raw, M)
        interleave(FIRST)
        quantize(w_codes, w_scales, w_bf)
        quantize_x(FIRST)
        nc.vector.transpose(out=b_turned[:], in_=b_rows[:])
        interleave(LAST)
        mix(FIRST, range(G))
        exp(FIRST, FIRST, range(G))
        interleave(MIDDLE_A)
        quantize_x(LAST)
        mix(LAST, range(G))
        exp(LAST, LAST, range(G))
        interleave(MIDDLE_B)
        others, final = range(G - 1), [G - 1]
        quantize_x(MIDDLE_A)
        mix(MIDDLE_A, reversed(range(G)))
        exp(MIDDLE_A, MIDDLE_A, final)
        quantize_x(MIDDLE_B)
        mix(MIDDLE_B, range(G))
        exp(MIDDLE_A, MIDDLE_B, others)
        exp(MIDDLE_B, MIDDLE_B, final)

        nc.vector.tensor_scalar(out=knee_tw_col[:], in0=tw_col[:], scalar1=KNEE, scalar2=None, op0=ALU.mult)
        cap(0, CW)
        nc.vector.reciprocal(out=inv_col[:], in_=knee_tw_col[:])
        for g in range(G):
            high(g, SPLIT, N)
        cap(SPLIT, N)
        for g in range(G - 1):
            high(g, 0, SPLIT)
        cap(CW, SPLIT)
        high(G - 1, 0, SPLIT)

        for g in range(G):
            for lo in (0, HALF):
                hi = lo + HALF
                nc.scalar.activation(out=ln[:, g, lo:hi], in_=e_capped[:, g, lo:hi], func=ACT.Ln, bias=one[:], scale=1.0)
                nc.vector.scalar_tensor_tensor(
                    out=y[:, g, lo:hi], in0=ln[:, g, lo:hi], scalar=inv_col[:], in1=v_high[:, g, lo:hi], op0=ALU.mult, op1=ALU.mult
                )
                if hi % STORE_COLS[g] == 0:
                    nc.sync.dma_start(out=out[g, :, hi - STORE_COLS[g] : hi], in_=y[:, g, hi - STORE_COLS[g] : hi])
